import numpy as np
import ml_dtypes


def mxq(x, axis, fmt="e4m3"):
    dtype, down = {"e4m3": (ml_dtypes.float8_e4m3fn, 7), "e5m2": (ml_dtypes.float8_e5m2, 14)}[fmt]
    v = np.moveaxis(np.asarray(x, np.float32).astype(ml_dtypes.bfloat16).astype(np.float64), axis, -1)
    blocks = v.reshape(v.shape[:-1] + (-1, 32))
    amax = np.abs(blocks).max(-1, keepdims=True)
    byte = np.maximum(np.where(amax > 0, np.frexp(amax)[1] - 1 + 127, 0) - down, 1)
    scale = np.exp2(byte - 127.0)
    codes = (blocks / scale).astype(np.float32).astype(dtype).astype(np.float64)
    return np.moveaxis((codes * scale).reshape(v.shape), -1, axis)


WIDE = False


def mx_kscale(k):
    if not WIDE:
        return np.ones(k)
    levels = np.array([10, -10, 5, -5, 0])
    if k % 512:
        return np.exp2(np.random.permutation(np.resize(levels, k // 32))).repeat(32)
    a = np.empty((k // 512, 16))
    for p in range(k // 512):
        a[p, :8] = np.random.permutation(np.resize(levels, 8))
        for g in range(8):
            far = levels[np.abs(levels - a[p, g]) >= 10]
            a[p, g + 8] = far[np.random.randint(len(far))]
    return np.exp2(a.ravel()).repeat(32)


def f64(x):
    return np.asarray(x).astype(np.float64)


def striped(idx):
    return np.tile(idx.reshape(-1, 16).T, (8, 1)).astype(np.uint16)


def unstriped(offs):
    return offs[:16].T.reshape(-1).astype(np.int64)


E2M1 = np.array([0.0, 0.5, 1.0, 1.5, 2.0, 3.0, 4.0, 6.0, -0.0, -0.5, -1.0, -1.5, -2.0, -3.0, -4.0, -6.0])


def pack_weight(w, fmt):
    k, n = w.shape
    w = f64(np.asarray(w, np.float32).astype(ml_dtypes.bfloat16)).reshape(k // 32, 32, n)
    amax = np.abs(w).max(1)
    if fmt == "e4m3":
        byte = np.frexp(amax)[1] - 1 + 127 - 7
    else:
        mant, ex = np.frexp(amax / 6.0)
        byte = np.where(mant > 0.5, ex, ex - 1) + 127
    byte = np.clip(np.where(amax > 0, byte, 1), 1, 254)
    scaled = (w * np.exp2(127.0 - byte)[:, None, :]).reshape(k, n).astype(np.float32)
    by_word = np.ascontiguousarray(scaled.reshape(k // 512, 128, 4, n).transpose(0, 1, 3, 2))
    if fmt == "e4m3":
        words = by_word.astype(ml_dtypes.float8_e4m3fn).view(np.uint8)
    else:
        c = by_word.astype(ml_dtypes.float4_e2m1fn).view(np.uint8) & 0xF
        words = (c[..., 0::2] | (c[..., 1::2] << 4)).reshape(k // 512, 128, 2 * n)
    return np.ascontiguousarray(words), np.ascontiguousarray(byte.astype(np.uint8).reshape(k // 512, 16, n))


def unpack_weight(words, scales, fmt):
    g, _, n = scales.shape
    words = np.ascontiguousarray(words).reshape(g, 128, n, -1)
    if fmt == "e4m3":
        vals = words.view(ml_dtypes.float8_e4m3fn).astype(np.float64)
    else:
        nib = np.empty((g, 128, n, 4), np.uint8)
        nib[..., 0::2] = words & 0xF
        nib[..., 1::2] = words >> 4
        vals = E2M1[nib]
    vals = vals * np.repeat(np.exp2(scales.astype(np.float64) - 127.0), 8, axis=1)[..., None]
    return vals.transpose(0, 1, 3, 2).reshape(g * 512, n)


def gelu(v):
    return 0.5 * v * (1.0 + np.tanh(np.sqrt(2.0 / np.pi) * (v + 0.044715 * v**3)))


K, T, E, C, N = 2048, 640, 10, 128, 128


def by_expert(wq, xq):
    return np.concatenate([wq[e].T @ xq[:, e * C:(e + 1) * C] for e in range(E)], axis=1)


def setup_inputs():
    n = np.random.standard_normal
    s = mx_kscale(K)[:, None]
    first = np.random.permutation(np.repeat(np.arange(E), T // E))
    second = (first + 1 + np.random.permutation(np.repeat(np.arange(E - 1), -(-T // (E - 1)))[:T])) % E
    while np.bincount(second, minlength=E).max() != T // E:
        load = np.bincount(second, minlength=E); hi, lo = int(load.argmax()), int(load.argmin())
        t = np.flatnonzero((second == hi) & (first != lo))[0]; second[t] = lo
    slot_token = np.empty(E * C, np.int64); pos = np.empty((2, T), np.int64); fill = np.zeros(E, np.int64)
    place = np.stack([np.random.permutation(C) for _ in range(E)])
    for r, deal in enumerate((first, second)):
        for t in np.random.permutation(T):
            e = deal[t]; j = e * C + place[e, fill[e]]; fill[e] += 1; slot_token[j] = t; pos[r, t] = j
    g = np.random.uniform(0.2, 0.8, T)
    w = [pack_weight(m, "e2m1") for m in n((E + 1, K, N)) / np.sqrt(K) / s[None]]
    return {
        "xT": (n((K, T)) * s).astype(np.float32),
        "w_words": np.stack([m[0] for m in w]),
        "w_scales": np.stack([m[1] for m in w]),
        "b": (0.3 * n((N, E + 1))).astype(np.float32),
        "gate": np.stack([np.tile(g, (N, 1)), np.tile(1.0 - g, (N, 1))]).astype(np.float32),
        "offs": striped(slot_token),
        "pos1": striped(pos[0]),
        "pos2": striped(pos[1]),
    }


def reference(xT, w_words, w_scales, b, gate, offs, pos1, pos2):
    idx = unstriped(offs)
    w = np.stack([unpack_weight(w_words[e], w_scales[e], "e2m1") for e in range(E + 1)])
    wq = w
    xs = mxq(f64(xT), 0, "e4m3")
    ys = gelu((wq[E].T @ xs) + f64(b)[:, E:])
    xq = mxq(f64(xT)[:, idx], 0, "e4m3")
    y = by_expert(w, xq)
    y = gelu(y + np.repeat(f64(b)[:, :E], C, axis=1))
    return ys + f64(gate[0]) * y[:, unstriped(pos1)] + f64(gate[1]) * y[:, unstriped(pos2)]

@@ -1,0 +1,206 @@
+from contextlib import ExitStack
+
+import concourse.mybir as mybir
+
+K, T, E, C, N = 2048, 640, 10, 128, 128
+S = E * C
+P = 128
+PASSES = 4
+FLOPS = 2 * K * N * (S + T)
+
+F32 = mybir.dt.float32
+BF16 = mybir.dt.bfloat16
+U32 = mybir.dt.uint32
+I32 = mybir.dt.int32
+U16 = mybir.dt.uint16
+U8 = mybir.dt.uint8
+FP8X4 = mybir.dt.float8_e4m3fn_x4
+FP4X4 = mybir.dt.float4_e2m1fn_x4
+GELU = mybir.ActivationFunctionType.Gelu_apprx_tanh
+MULT = mybir.AluOpType.mult
+
+PIECES = [(0, 384), (384, 384), (768, 256), (1024, 256)]
+
+
+def quant_cuts(start, size):
+    cuts = []
+    while size:
+        w = 256 if size >= 256 else 128
+        cuts.append((start, w))
+        start += w
+        size -= w
+    return cuts
+
+
+def tile_moe_shr_lin_gelu_kernel(tc, xT, w_words, w_scales, b, gate, offs, pos1, pos2, out):
+    nc = tc.nc
+    with ExitStack() as ctx:
+        keep = ctx.enter_context(tc.tile_pool(name="keep", bufs=1))
+        psum = ctx.enter_context(tc.psum_pool(name="psum", bufs=1))
+
+        offs_t = keep.tile([P, S // 16], U16, name="offs_t")
+        pos1_t = keep.tile([P, T // 16], U16, name="pos1_t")
+        pos2_t = keep.tile([P, T // 16], U16, name="pos2_t")
+        bias = keep.tile([P, E + 1], F32, name="bias")
+        gates = keep.tile([P, 2 * T], F32, name="gates")
+        wsc = keep.tile([P, (E + 1) * PASSES * N], U8, name="wsc", align_bytes=64)
+        warm = keep.tile([P, 8], F32, name="warm")
+        y = keep.tile([P, S], F32, name="y")
+        ys = keep.tile([P, T], F32, name="ys")
+        words, raw, pairs, gath, slots, shq, cs, ss, csh, ssh = [], [], [], [], [], [], [], [], [], []
+        for a in range(PASSES):
+            words.append(keep.tile([P, (E + 1) * 2 * N], U8, name=f"words{a}", align_bytes=64))
+            raw.append([keep.tile([P, 2, T], F32, name=f"raw{a}{h}") for h in range(2)])
+            pairs.append(keep.tile([P, 4 * T], BF16, name=f"pairs{a}", align_bytes=64))
+            gath.append(keep.tile([P, 4 * S], BF16, name=f"gath{a}", align_bytes=64))
+            slots.append(keep.tile([P, 4 * S], BF16, name=f"slots{a}", align_bytes=64))
+            shq.append(keep.tile([P, 4 * T], BF16, name=f"shq{a}", align_bytes=64))
+            cs.append(keep.tile([P, S], U32, name=f"cs{a}", align_bytes=64))
+            ss.append(keep.tile([P, S], U8, name=f"ss{a}", align_bytes=64))
+            csh.append(keep.tile([P, T], U32, name=f"csh{a}", align_bytes=64))
+            ssh.append(keep.tile([P, T], U8, name=f"ssh{a}", align_bytes=64))
+
+        xv = xT.rearrange("(a p j) t -> a p j t", p=P, j=4)
+        wv = w_words.bitcast(I32)
+        sv = w_scales.bitcast(I32)
+
+        nc.vector.memset(warm[:], 0.0)
+        nc.scalar.activation(out=warm[:], in_=warm[:], func=GELU)
+        nc.vector.memset(wsc[:].bitcast(I32), 0)
+
+        def load_x(a, h):
+            nc.sync.dma_start(raw[a][h][:], xv[a][:, 2 * h : 2 * h + 2, :])
+
+        def load_w(a):
+            nc.sync.dma_start(
+                words[a][:].bitcast(I32).rearrange("p (e n) -> p e n", e=E + 1),
+                wv[:, a, :, :].rearrange("e p n -> p e n"),
+            )
+
+        load_x(0, 0)
+        nc.sync.dma_start(offs_t[:], offs)
+        load_x(0, 1)
+        load_x(1, 0)
+        load_x(1, 1)
+        for q in range(4):
+            nc.sync.dma_start(
+                wsc[32 * q : 32 * q + 4, :].bitcast(I32).rearrange("q (i n) -> q i n", n=N // 4),
+                sv[:, :, 4 * q : 4 * q + 4, :].rearrange("e a q n -> q (e a) n"),
+            )
+        load_w(0)
+        load_w(1)
+        load_x(2, 0)
+        load_x(2, 1)
+        load_w(2)
+        load_x(3, 0)
+        load_x(3, 1)
+        load_w(3)
+        nc.sync.dma_start(bias[:], b)
+        nc.sync.dma_start(pos1_t[:], pos1)
+        nc.sync.dma_start(pos2_t[:], pos2)
+        nc.sync.dma_start(gates[:].rearrange("p (g t) -> p g t", g=2), gate.rearrange("g p t -> p g t"))
+
+        def cast(a, h):
+            nc.scalar.copy(
+                out=pairs[a][:, 2 * T * h : 2 * T * (h + 1)].rearrange("p (t e) -> p t e", e=2),
+                in_=raw[a][h][:].rearrange("p e t -> p t e"),
+            )
+
+        def gather(a, h, start, size):
+            nc.vector.tensor_copy(
+                gath[a][:].bitcast(U32)[:, S * h + start : S * h + start + size],
+                pairs[a][:].bitcast(U32)[:, T * h : T * (h + 1)].indirect(offs_t[:, start // 16 : (start + size) // 16]),
+            )
+
+        def weave(a, start, size):
+            nc.scalar.copy(
+                out=slots[a][:].bitcast(U32).rearrange("p (n u) -> p n u", u=2)[:, start : start + size, :],
+                in_=gath[a][:].bitcast(U32).rearrange("p (u n) -> p n u", u=2)[:, start : start + size, :],
+            )
+
+        def weave_shared(a):
+            nc.scalar.copy(
+                out=shq[a][:].bitcast(U32).rearrange("p (n u) -> p n u", u=2),
+                in_=pairs[a][:].bitcast(U32).rearrange("p (u n) -> p n u", u=2),
+            )
+
+        def quant(a, start, size):
+            for s0, w in quant_cuts(start, size):
+                nc.vector.quantize_mx(
+                    out=cs[a][:, s0 : s0 + w].bitcast(FP8X4),
+                    scales=ss[a][:, s0 : s0 + w],
+                    in_=slots[a][:, 4 * s0 : 4 * (s0 + w)],
+                )
+
+        def quant_shared(a):
+            for s0, w in ((0, 512), (512, 128)):
+                nc.vector.quantize_mx(
+                    out=csh[a][:, s0 : s0 + w].bitcast(FP8X4),
+                    scales=ssh[a][:, s0 : s0 + w],
+                    in_=shq[a][:, 4 * s0 : 4 * (s0 + w)],
+                )
+
+        def multiply(bank, e, codes, scales, s0, w):
+            for a in range(PASSES):
+                i = e * PASSES + a
+                nc.tensor.matmul_mx(
+                    out=bank,
+                    lhsT=words[a][:, e * 2 * N : (e + 1) * 2 * N].bitcast(FP4X4),
+                    lhsT_scale=wsc[:, i * N : (i + 1) * N],
+                    rhs=codes[a][:, s0 : s0 + w].bitcast(FP8X4),
+                    rhs_scale=scales[a][:, s0 : s0 + w],
+                    start=(a == 0),
+                    stop=(a == PASSES - 1),
+                )
+
+        def expert(e):
+            bank = psum.tile([P, C], F32, name=f"bank{e % 6}")
+            multiply(bank[:], e, cs, ss, e * C, C)
+            nc.scalar.activation(out=y[:, e * C : (e + 1) * C], in_=bank[:], func=GELU, bias=bias[:, e : e + 1])
+
+        def shared():
+            for s0, w in ((0, 512), (512, 128)):
+                bank = psum.tile([P, w], F32, name=f"shared{s0}")
+                multiply(bank[:], E, csh, ssh, s0, w)
+                nc.scalar.activation(out=ys[:, s0 : s0 + w], in_=bank[:], func=GELU, bias=bias[:, E : E + 1])
+
+        cast(0, 0)
+        cast(0, 1)
+        pending = []
+
+        def finish(a, start, size):
+            quant(a, start, size)
+            if a == PASSES - 1:
+                for e in range(start // C, (start + size) // C):
+                    expert(e)
+
+        for a in range(PASSES):
+            for i, (start, size) in enumerate(PIECES):
+                gather(a, 0, start, size)
+                gather(a, 1, start, size)
+                weave(a, start, size)
+                if pending:
+                    finish(*pending.pop())
+                pending.append((a, start, size))
+                if i == 0:
+                    weave_shared(a)
+                if i == 1:
+                    quant_shared(a)
+                    if a == PASSES - 1:
+                        shared()
+                if i < 2 and a < PASSES - 1:
+                    cast(a + 1, i)
+        finish(*pending.pop())
+
+        s1 = keep.tile([P, T], F32, name="s1")
+        s2 = keep.tile([P, T], F32, name="s2")
+        t1 = keep.tile([P, T], F32, name="t1")
+        res = keep.tile([P, T], F32, name="res")
+        half = T // 2
+        for c0 in (0, half):
+            cols = slice(c0, c0 + half)
+            nc.vector.tensor_tensor(s1[:, cols], y[:].indirect(pos1_t[:, c0 // 16 : (c0 + half) // 16]), gates[:, c0 : c0 + half], MULT)
+            nc.vector.tensor_tensor(s2[:, cols], y[:].indirect(pos2_t[:, c0 // 16 : (c0 + half) // 16]), gates[:, T + c0 : T + c0 + half], MULT)
+            nc.vector.tensor_add(t1[:, cols], s1[:, cols], ys[:, cols])
+            nc.vector.tensor_add(res[:, cols], t1[:, cols], s2[:, cols])
+            nc.sync.dma_start(out[:, cols], res[:, cols])

@@ -19,17 +19,8 @@ FP4X4 = mybir.dt.float4_e2m1fn_x4
 GELU = mybir.ActivationFunctionType.Gelu_apprx_tanh
 MULT = mybir.AluOpType.mult
 
-PIECES = [(0, 384), (384, 384), (768, 256), (1024, 256)]
-
-
-def quant_cuts(start, size):
-    cuts = []
-    while size:
-        w = 256 if size >= 256 else 128
-        cuts.append((start, w))
-        start += w
-        size -= w
-    return cuts
+PIECES = [((0, 480), [(0, 256)]), ((480, 480), [(256, 512)]), ((960, 320), [(768, 512)])]
+LAST = [((0, 480), [(0, 256)]), ((480, 480), [(256, 512)]), ((960, 192), [(768, 256), (1024, 128)]), ((1152, 128), [(1152, 128)])]
 
 
 def tile_moe_shr_lin_gelu_kernel(tc, xT, w_words, w_scales, b, gate, offs, pos1, pos2, out):
@@ -54,11 +45,14 @@ def tile_moe_shr_lin_gelu_kernel(tc, xT, w_words, w_scales, b, gate, offs, pos1,
             pairs.append(keep.tile([P, 4 * T], BF16, name=f"pairs{a}", align_bytes=64))
             gath.append(keep.tile([P, 4 * S], BF16, name=f"gath{a}", align_bytes=64))
             slots.append(keep.tile([P, 4 * S], BF16, name=f"slots{a}", align_bytes=64))
-            shq.append(keep.tile([P, 4 * T], BF16, name=f"shq{a}", align_bytes=64))
+            shq.append(keep.tile([P, 4 * 512], BF16, name=f"shq{a}", align_bytes=64))
             cs.append(keep.tile([P, S], U32, name=f"cs{a}", align_bytes=64))
             ss.append(keep.tile([P, S], U8, name=f"ss{a}", align_bytes=64))
-            csh.append(keep.tile([P, T], U32, name=f"csh{a}", align_bytes=64))
-            ssh.append(keep.tile([P, T], U8, name=f"ssh{a}", align_bytes=64))
+            csh.append(keep.tile([P, 512], U32, name=f"csh{a}", align_bytes=64))
+            ssh.append(keep.tile([P, 512], U8, name=f"ssh{a}", align_bytes=64))
+        rest = keep.tile([P, PASSES * 4 * C], BF16, name="rest", align_bytes=64)
+        crest = keep.tile([P, PASSES * C], U32, name="crest", align_bytes=64)
+        srest = keep.tile([P, PASSES * C], U8, name="srest", align_bytes=64)
 
         xv = xT.rearrange("(a p j) t -> a p j t", p=P, j=4)
         wv = w_words.bitcast(I32)
@@ -69,7 +63,8 @@ def tile_moe_shr_lin_gelu_kernel(tc, xT, w_words, w_scales, b, gate, offs, pos1,
         nc.vector.memset(wsc[:].bitcast(I32), 0)
 
         def load_x(a, h):
-            nc.sync.dma_start(raw[a][h][:], xv[a][:, 2 * h : 2 * h + 2, :])
+            for c0, c1 in ((0, T // 2), (T // 2, T)) if (a, h) == (0, 0) else ((0, T),):
+                nc.sync.dma_start(raw[a][h][:, :, c0:c1], xv[a][:, 2 * h : 2 * h + 2, c0:c1])
 
         def load_w(a):
             nc.sync.dma_start(
@@ -82,28 +77,28 @@ def tile_moe_shr_lin_gelu_kernel(tc, xT, w_words, w_scales, b, gate, offs, pos1,
         load_x(0, 1)
         load_x(1, 0)
         load_x(1, 1)
+        load_x(2, 0)
+        load_x(2, 1)
         for q in range(4):
             nc.sync.dma_start(
                 wsc[32 * q : 32 * q + 4, :].bitcast(I32).rearrange("q (i n) -> q i n", n=N // 4),
                 sv[:, :, 4 * q : 4 * q + 4, :].rearrange("e a q n -> q (e a) n"),
             )
         load_w(0)
-        load_w(1)
-        load_x(2, 0)
-        load_x(2, 1)
-        load_w(2)
         load_x(3, 0)
         load_x(3, 1)
+        load_w(1)
+        load_w(2)
         load_w(3)
         nc.sync.dma_start(bias[:], b)
         nc.sync.dma_start(pos1_t[:], pos1)
         nc.sync.dma_start(pos2_t[:], pos2)
         nc.sync.dma_start(gates[:].rearrange("p (g t) -> p g t", g=2), gate.rearrange("g p t -> p g t"))
 
-        def cast(a, h):
-            nc.scalar.copy(
-                out=pairs[a][:, 2 * T * h : 2 * T * (h + 1)].rearrange("p (t e) -> p t e", e=2),
-                in_=raw[a][h][:].rearrange("p e t -> p t e"),
+        def cast(a, h, c0=0, c1=T, copy=nc.scalar.copy):
+            copy(
+                out=pairs[a][:, 2 * T * h : 2 * T * (h + 1)].rearrange("p (t e) -> p t e", e=2)[:, c0:c1, :],
+                in_=raw[a][h][:, :, c0:c1].rearrange("p e t -> p t e"),
             )
 
         def gather(a, h, start, size):
@@ -119,13 +114,14 @@ def tile_moe_shr_lin_gelu_kernel(tc, xT, w_words, w_scales, b, gate, offs, pos1,
             )
 
         def weave_shared(a):
+            src = pairs[a][:].bitcast(U32).rearrange("p (u n) -> p n u", u=2)
+            nc.scalar.copy(out=shq[a][:].bitcast(U32).rearrange("p (n u) -> p n u", u=2), in_=src[:, :512, :])
             nc.scalar.copy(
-                out=shq[a][:].bitcast(U32).rearrange("p (n u) -> p n u", u=2),
-                in_=pairs[a][:].bitcast(U32).rearrange("p (u n) -> p n u", u=2),
+                out=rest[:].bitcast(U32)[:, 2 * C * a : 2 * C * (a + 1)].rearrange("p (n u) -> p n u", u=2), in_=src[:, 512:, :]
             )
 
-        def quant(a, start, size):
-            for s0, w in quant_cuts(start, size):
+        def quant(a, cuts):
+            for s0, w in cuts:
                 nc.vector.quantize_mx(
                     out=cs[a][:, s0 : s0 + w].bitcast(FP8X4),
                     scales=ss[a][:, s0 : s0 + w],
@@ -133,12 +129,10 @@ def tile_moe_shr_lin_gelu_kernel(tc, xT, w_words, w_scales, b, gate, offs, pos1,
                 )
 
         def quant_shared(a):
-            for s0, w in ((0, 512), (512, 128)):
-                nc.vector.quantize_mx(
-                    out=csh[a][:, s0 : s0 + w].bitcast(FP8X4),
-                    scales=ssh[a][:, s0 : s0 + w],
-                    in_=shq[a][:, 4 * s0 : 4 * (s0 + w)],
-                )
+            nc.vector.quantize_mx(out=csh[a][:].bitcast(FP8X4), scales=ssh[a][:], in_=shq[a][:])
+
+        def quant_rest():
+            nc.vector.quantize_mx(out=crest[:].bitcast(FP8X4), scales=srest[:], in_=rest[:])
 
         def multiply(bank, e, codes, scales, s0, w):
             for a in range(PASSES):
@@ -147,57 +141,60 @@ def tile_moe_shr_lin_gelu_kernel(tc, xT, w_words, w_scales, b, gate, offs, pos1,
                     out=bank,
                     lhsT=words[a][:, e * 2 * N : (e + 1) * 2 * N].bitcast(FP4X4),
                     lhsT_scale=wsc[:, i * N : (i + 1) * N],
-                    rhs=codes[a][:, s0 : s0 + w].bitcast(FP8X4),
-                    rhs_scale=scales[a][:, s0 : s0 + w],
+                    rhs=codes(a)[:, s0(a) : s0(a) + w].bitcast(FP8X4),
+                    rhs_scale=scales(a)[:, s0(a) : s0(a) + w],
                     start=(a == 0),
                     stop=(a == PASSES - 1),
                 )
 
         def expert(e):
-            bank = psum.tile([P, C], F32, name=f"bank{e % 6}")
-            multiply(bank[:], e, cs, ss, e * C, C)
+            bank = psum.tile([P, C], F32, name=f"bank{e if e > 5 else e % 2}")
+            multiply(bank[:], e, lambda a: cs[a], lambda a: ss[a], lambda a: e * C, C)
             nc.scalar.activation(out=y[:, e * C : (e + 1) * C], in_=bank[:], func=GELU, bias=bias[:, e : e + 1])
 
         def shared():
-            for s0, w in ((0, 512), (512, 128)):
-                bank = psum.tile([P, w], F32, name=f"shared{s0}")
-                multiply(bank[:], E, csh, ssh, s0, w)
-                nc.scalar.activation(out=ys[:, s0 : s0 + w], in_=bank[:], func=GELU, bias=bias[:, E : E + 1])
+            bank = psum.tile([P, 512], F32, name="bank_shared")
+            multiply(bank[:], E, lambda a: csh[a], lambda a: ssh[a], lambda a: 0, 512)
+            nc.scalar.activation(out=ys[:, :512], in_=bank[:], func=GELU, bias=bias[:, E : E + 1])
+            bank_rest = psum.tile([P, C], F32, name="bank_rest")
+            multiply(bank_rest[:], E, lambda a: crest, lambda a: srest, lambda a: a * C, C)
+            nc.scalar.activation(out=ys[:, 512:], in_=bank_rest[:], func=GELU, bias=bias[:, E : E + 1])
 
-        cast(0, 0)
+        cast(0, 0, 0, T // 2)
+        cast(0, 0, T // 2, T, nc.vector.tensor_copy)
         cast(0, 1)
         pending = []
 
-        def finish(a, start, size):
-            quant(a, start, size)
+        def finish(a, cuts):
+            quant(a, cuts)
             if a == PASSES - 1:
-                for e in range(start // C, (start + size) // C):
-                    expert(e)
+                for s0, w in cuts:
+                    for e in range(s0 // C, (s0 + w) // C):
+                        expert(e)
 
         for a in range(PASSES):
-            for i, (start, size) in enumerate(PIECES):
+            for i, ((start, size), cuts) in enumerate(LAST if a == PASSES - 1 else PIECES):
                 gather(a, 0, start, size)
                 gather(a, 1, start, size)
                 weave(a, start, size)
                 if pending:
                     finish(*pending.pop())
-                pending.append((a, start, size))
-                if i == 0:
-                    weave_shared(a)
-                if i == 1:
-                    quant_shared(a)
-                    if a == PASSES - 1:
-                        shared()
+                pending.append((a, cuts))
                 if i < 2 and a < PASSES - 1:
                     cast(a + 1, i)
+                if i == 2:
+                    weave_shared(a)
         finish(*pending.pop())
+        for a in range(PASSES):
+            quant_shared(a)
+        quant_rest()
+        shared()
 
         s1 = keep.tile([P, T], F32, name="s1")
         s2 = keep.tile([P, T], F32, name="s2")
         t1 = keep.tile([P, T], F32, name="t1")
         res = keep.tile([P, T], F32, name="res")
-        half = T // 2
-        for c0 in (0, half):
+        for c0, half in ((0, 512), (512, 128)):
             cols = slice(c0, c0 + half)
             nc.vector.tensor_tensor(s1[:, cols], y[:].indirect(pos1_t[:, c0 // 16 : (c0 + half) // 16]), gates[:, c0 : c0 + half], MULT)
             nc.vector.tensor_tensor(s2[:, cols], y[:].indirect(pos2_t[:, c0 // 16 : (c0 + half) // 16]), gates[:, T + c0 : T + c0 + half], MULT)

@@ -19,14 +19,17 @@ FP4X4 = mybir.dt.float4_e2m1fn_x4
 GELU = mybir.ActivationFunctionType.Gelu_apprx_tanh
 MULT = mybir.AluOpType.mult
 
-PIECES = [((0, 480), [(0, 256)]), ((480, 480), [(256, 512)]), ((960, 320), [(768, 512)])]
+NARROW = [((0, 480), [(0, 256)]), ((480, 480), [(256, 512)]), ((960, 320), [(768, 512)])]
+WIDE = [((0, 640), [(0, 512)]), ((640, 640), [(512, 512), (1024, 256)])]
 LAST = [((0, 480), [(0, 256)]), ((480, 480), [(256, 512)]), ((960, 192), [(768, 256), (1024, 128)]), ((1152, 128), [(1152, 128)])]
+PIECES = [NARROW, WIDE, WIDE, LAST]
 
 
 def tile_moe_shr_lin_gelu_kernel(tc, xT, w_words, w_scales, b, gate, offs, pos1, pos2, out):
     nc = tc.nc
     with ExitStack() as ctx:
         keep = ctx.enter_context(tc.tile_pool(name="keep", bufs=1))
+        ring = ctx.enter_context(tc.tile_pool(name="ring", bufs=2))
         psum = ctx.enter_context(tc.psum_pool(name="psum", bufs=1))
 
         offs_t = keep.tile([P, S // 16], U16, name="offs_t")
@@ -38,11 +41,9 @@ def tile_moe_shr_lin_gelu_kernel(tc, xT, w_words, w_scales, b, gate, offs, pos1,
         warm = keep.tile([P, 8], F32, name="warm")
         y = keep.tile([P, S], F32, name="y")
         ys = keep.tile([P, T], F32, name="ys")
-        words, raw, pairs, gath, slots, shq, cs, ss, csh, ssh = [], [], [], [], [], [], [], [], [], []
+        words, gath, slots, shq, cs, ss, csh, ssh = [], [], [], [], [], [], [], []
         for a in range(PASSES):
             words.append(keep.tile([P, (E + 1) * 2 * N], U8, name=f"words{a}", align_bytes=64))
-            raw.append([keep.tile([P, 2, T], F32, name=f"raw{a}{h}") for h in range(2)])
-            pairs.append(keep.tile([P, 4 * T], BF16, name=f"pairs{a}", align_bytes=64))
             gath.append(keep.tile([P, 4 * S], BF16, name=f"gath{a}", align_bytes=64))
             slots.append(keep.tile([P, 4 * S], BF16, name=f"slots{a}", align_bytes=64))
             shq.append(keep.tile([P, 4 * 512], BF16, name=f"shq{a}", align_bytes=64))
@@ -54,6 +55,9 @@ def tile_moe_shr_lin_gelu_kernel(tc, xT, w_words, w_scales, b, gate, offs, pos1,
         crest = keep.tile([P, PASSES * C], U32, name="crest", align_bytes=64)
         srest = keep.tile([P, PASSES * C], U8, name="srest", align_bytes=64)
 
+        pairs_all = keep.tile([P, PASSES * 4 * T], BF16, name="pairs_all", align_bytes=64)
+        pairs = [pairs_all[:, 4 * T * (PASSES - 1 - a) : 4 * T * (PASSES - a)] for a in range(PASSES)]
+
         xv = xT.rearrange("(a p j) t -> a p j t", p=P, j=4)
         wv = w_words.bitcast(I32)
         sv = w_scales.bitcast(I32)
@@ -62,9 +66,12 @@ def tile_moe_shr_lin_gelu_kernel(tc, xT, w_words, w_scales, b, gate, offs, pos1,
         nc.scalar.activation(out=warm[:], in_=warm[:], func=GELU)
         nc.vector.memset(wsc[:].bitcast(I32), 0)
 
+        raw = {}
+
         def load_x(a, h):
+            raw[a, h] = ring.tile([P, 2, T], F32, name=f"raw{h}")
             for c0, c1 in ((0, T // 2), (T // 2, T)) if (a, h) == (0, 0) else ((0, T),):
-                nc.sync.dma_start(raw[a][h][:, :, c0:c1], xv[a][:, 2 * h : 2 * h + 2, c0:c1])
+                nc.sync.dma_start(raw[a, h][:, :, c0:c1], xv[a][:, 2 * h : 2 * h + 2, c0:c1])
 
         def load_w(a):
             nc.sync.dma_start(
@@ -77,34 +84,37 @@ def tile_moe_shr_lin_gelu_kernel(tc, xT, w_words, w_scales, b, gate, offs, pos1,
         load_x(0, 1)
         load_x(1, 0)
         load_x(1, 1)
-        load_x(2, 0)
-        load_x(2, 1)
-        for q in range(4):
-            nc.sync.dma_start(
-                wsc[32 * q : 32 * q + 4, :].bitcast(I32).rearrange("q (i n) -> q i n", n=N // 4),
-                sv[:, :, 4 * q : 4 * q + 4, :].rearrange("e a q n -> q (e a) n"),
-            )
-        load_w(0)
-        load_x(3, 0)
-        load_x(3, 1)
-        load_w(1)
-        load_w(2)
-        load_w(3)
-        nc.sync.dma_start(bias[:], b)
-        nc.sync.dma_start(pos1_t[:], pos1)
-        nc.sync.dma_start(pos2_t[:], pos2)
-        nc.sync.dma_start(gates[:].rearrange("p (g t) -> p g t", g=2), gate.rearrange("g p t -> p g t"))
+
+        def load_rest():
+            load_x(2, 0)
+            load_x(2, 1)
+            for q in range(4):
+                nc.sync.dma_start(
+                    wsc[32 * q : 32 * q + 4, :].bitcast(I32).rearrange("q (i n) -> q i n", n=N // 4),
+                    sv[:, :, 4 * q : 4 * q + 4, :].rearrange("e a q n -> q (e a) n"),
+                )
+            load_w(0)
+            load_x(3, 0)
+            load_x(3, 1)
+            load_w(1)
+            load_w(2)
+            load_w(3)
+            nc.sync.dma_start(bias[:], b)
+            nc.sync.dma_start(pos1_t[:], pos1)
+            nc.sync.dma_start(pos2_t[:], pos2)
+            nc.sync.dma_start(gates[:].rearrange("p (g t) -> p g t", g=2), gate.rearrange("g p t -> p g t"))
 
         def cast(a, h, c0=0, c1=T, copy=nc.scalar.copy):
             copy(
                 out=pairs[a][:, 2 * T * h : 2 * T * (h + 1)].rearrange("p (t e) -> p t e", e=2)[:, c0:c1, :],
-                in_=raw[a][h][:, :, c0:c1].rearrange("p e t -> p t e"),
+                in_=raw[a, h][:, :, c0:c1].rearrange("p e t -> p t e"),
             )
 
         def gather(a, h, start, size):
+            window = 2 * T * (PASSES - 1 - a) + T * h
             nc.vector.tensor_copy(
                 gath[a][:].bitcast(U32)[:, S * h + start : S * h + start + size],
-                pairs[a][:].bitcast(U32)[:, T * h : T * (h + 1)].indirect(offs_t[:, start // 16 : (start + size) // 16]),
+                pairs_all[:].bitcast(U32)[:, window : window + (T if size < T else 2 * T)].indirect(offs_t[:, start // 16 : (start + size) // 16]),
             )
 
         def weave(a, start, size):
@@ -114,7 +124,7 @@ def tile_moe_shr_lin_gelu_kernel(tc, xT, w_words, w_scales, b, gate, offs, pos1,
             )
 
         def weave_shared(a):
-            src = pairs[a][:].bitcast(U32).rearrange("p (u n) -> p n u", u=2)
+            src = pairs[a].bitcast(U32).rearrange("p (u n) -> p n u", u=2)
             nc.scalar.copy(out=shq[a][:].bitcast(U32).rearrange("p (n u) -> p n u", u=2), in_=src[:, :512, :])
             nc.scalar.copy(
                 out=rest[:].bitcast(U32)[:, 2 * C * a : 2 * C * (a + 1)].rearrange("p (n u) -> p n u", u=2), in_=src[:, 512:, :]
@@ -147,42 +157,55 @@ def tile_moe_shr_lin_gelu_kernel(tc, xT, w_words, w_scales, b, gate, offs, pos1,
                     stop=(a == PASSES - 1),
                 )
 
-        def expert(e):
-            bank = psum.tile([P, C], F32, name=f"bank{e if e > 5 else e % 2}")
-            multiply(bank[:], e, lambda a: cs[a], lambda a: ss[a], lambda a: e * C, C)
-            nc.scalar.activation(out=y[:, e * C : (e + 1) * C], in_=bank[:], func=GELU, bias=bias[:, e : e + 1])
+        banks = {}
+
+        def bank_of(e):
+            key = e if e > 5 else e // 2
+            if key not in banks:
+                banks[key] = psum.tile([P, 3 * C if key == 0 else 2 * C if key < 3 else C], F32, name=f"bank{key}")
+            at = e % 2 * C if key < 3 else 0
+            return banks[key][:, at : at + C]
+
+        def experts(group):
+            for e in group:
+                multiply(bank_of(e), e, lambda a: cs[a], lambda a: ss[a], lambda a: e * C, C)
+            for e in group:
+                nc.scalar.activation(out=y[:, e * C : (e + 1) * C], in_=bank_of(e), func=GELU, bias=bias[:, e : e + 1])
 
         def shared():
             bank = psum.tile([P, 512], F32, name="bank_shared")
             multiply(bank[:], E, lambda a: csh[a], lambda a: ssh[a], lambda a: 0, 512)
             nc.scalar.activation(out=ys[:, :512], in_=bank[:], func=GELU, bias=bias[:, E : E + 1])
-            bank_rest = psum.tile([P, C], F32, name="bank_rest")
-            multiply(bank_rest[:], E, lambda a: crest, lambda a: srest, lambda a: a * C, C)
-            nc.scalar.activation(out=ys[:, 512:], in_=bank_rest[:], func=GELU, bias=bias[:, E : E + 1])
+            bank_rest = banks[0][:, 2 * C :]
+            multiply(bank_rest, E, lambda a: crest, lambda a: srest, lambda a: a * C, C)
+            nc.scalar.activation(out=ys[:, 512:], in_=bank_rest, func=GELU, bias=bias[:, E : E + 1])
 
-        cast(0, 0, 0, T // 2)
+        cast(0, 0, 0, T // 2, nc.vector.tensor_copy)
         cast(0, 0, T // 2, T, nc.vector.tensor_copy)
         cast(0, 1)
+        cast(1, 0)
+        cast(1, 1)
+        load_rest()
         pending = []
 
         def finish(a, cuts):
             quant(a, cuts)
             if a == PASSES - 1:
                 for s0, w in cuts:
-                    for e in range(s0 // C, (s0 + w) // C):
-                        expert(e)
+                    experts(range(s0 // C, (s0 + w) // C))
 
         for a in range(PASSES):
-            for i, ((start, size), cuts) in enumerate(LAST if a == PASSES - 1 else PIECES):
+            if 0 < a < PASSES - 1:
+                cast(a + 1, 0)
+                cast(a + 1, 1)
+            for i, ((start, size), cuts) in enumerate(PIECES[a]):
                 gather(a, 0, start, size)
                 gather(a, 1, start, size)
                 weave(a, start, size)
                 if pending:
                     finish(*pending.pop())
                 pending.append((a, cuts))
-                if i < 2 and a < PASSES - 1:
-                    cast(a + 1, i)
-                if i == 2:
+                if i == min(len(PIECES[a]) - 1, 2):
                     weave_shared(a)
         finish(*pending.pop())
         for a in range(PASSES):
@@ -194,10 +217,10 @@ def tile_moe_shr_lin_gelu_kernel(tc, xT, w_words, w_scales, b, gate, offs, pos1,
         s2 = keep.tile([P, T], F32, name="s2")
         t1 = keep.tile([P, T], F32, name="t1")
         res = keep.tile([P, T], F32, name="res")
-        for c0, half in ((0, 512), (512, 128)):
-            cols = slice(c0, c0 + half)
-            nc.vector.tensor_tensor(s1[:, cols], y[:].indirect(pos1_t[:, c0 // 16 : (c0 + half) // 16]), gates[:, c0 : c0 + half], MULT)
-            nc.vector.tensor_tensor(s2[:, cols], y[:].indirect(pos2_t[:, c0 // 16 : (c0 + half) // 16]), gates[:, T + c0 : T + c0 + half], MULT)
-            nc.vector.tensor_add(t1[:, cols], s1[:, cols], ys[:, cols])
-            nc.vector.tensor_add(res[:, cols], t1[:, cols], s2[:, cols])
+        nc.vector.tensor_tensor(s1[:], y[:].indirect(pos1_t[:]), gates[:, :T], MULT)
+        nc.vector.tensor_tensor(s2[:], y[:].indirect(pos2_t[:]), gates[:, T:], MULT)
+        nc.vector.tensor_add(t1[:], s1[:], s2[:])
+        for c0, size in ((0, 512), (512, 128)):
+            cols = slice(c0, c0 + size)
+            nc.vector.tensor_add(res[:, cols], t1[:, cols], ys[:, cols])
             nc.sync.dma_start(out[:, cols], res[:, cols])

@@ -70,8 +70,7 @@ def tile_moe_shr_lin_gelu_kernel(tc, xT, w_words, w_scales, b, gate, offs, pos1,
 
         def load_x(a, h):
             raw[a, h] = ring.tile([P, 2, T], F32, name=f"raw{h}")
-            for c0, c1 in ((0, T // 2), (T // 2, T)) if (a, h) == (0, 0) else ((0, T),):
-                nc.sync.dma_start(raw[a, h][:, :, c0:c1], xv[a][:, 2 * h : 2 * h + 2, c0:c1])
+            nc.sync.dma_start(raw[a, h][:], xv[a][:, 2 * h : 2 * h + 2, :])
 
         def load_w(a):
             nc.sync.dma_start(
@@ -180,8 +179,8 @@ def tile_moe_shr_lin_gelu_kernel(tc, xT, w_words, w_scales, b, gate, offs, pos1,
             multiply(bank_rest, E, lambda a: crest, lambda a: srest, lambda a: a * C, C)
             nc.scalar.activation(out=ys[:, 512:], in_=bank_rest, func=GELU, bias=bias[:, E : E + 1])
 
-        cast(0, 0, 0, T // 2, nc.vector.tensor_copy)
-        cast(0, 0, T // 2, T, nc.vector.tensor_copy)
+        cast(0, 0, 0, 384, nc.vector.tensor_copy)
+        cast(0, 0, 384, T)
         cast(0, 1)
         cast(1, 0)
         cast(1, 1)
@@ -219,8 +218,9 @@ def tile_moe_shr_lin_gelu_kernel(tc, xT, w_words, w_scales, b, gate, offs, pos1,
         res = keep.tile([P, T], F32, name="res")
         nc.vector.tensor_tensor(s1[:], y[:].indirect(pos1_t[:]), gates[:, :T], MULT)
         nc.vector.tensor_tensor(s2[:], y[:].indirect(pos2_t[:]), gates[:, T:], MULT)
-        nc.vector.tensor_add(t1[:], s1[:], s2[:])
-        for c0, size in ((0, 512), (512, 128)):
-            cols = slice(c0, c0 + size)
-            nc.vector.tensor_add(res[:, cols], t1[:, cols], ys[:, cols])
+        parts = (slice(0, 384), slice(384, T))
+        for cols in parts:
+            nc.vector.tensor_add(t1[:, cols], s1[:, cols], ys[:, cols])
+        for cols in parts:
+            nc.vector.tensor_add(res[:, cols], t1[:, cols], s2[:, cols])
             nc.sync.dma_start(out[:, cols], res[:, cols])

from contextlib import ExitStack

import concourse.mybir as mybir

K, T, E, C, N = 2048, 640, 10, 128, 128
S = E * C
P = 128
PASSES = 4
FLOPS = 2 * K * N * (S + T)

F32 = mybir.dt.float32
BF16 = mybir.dt.bfloat16
U32 = mybir.dt.uint32
I32 = mybir.dt.int32
U16 = mybir.dt.uint16
U8 = mybir.dt.uint8
FP8X4 = mybir.dt.float8_e4m3fn_x4
FP4X4 = mybir.dt.float4_e2m1fn_x4
GELU = mybir.ActivationFunctionType.Gelu_apprx_tanh
MULT = mybir.AluOpType.mult

NARROW = [((0, 480), [(0, 256)]), ((480, 480), [(256, 512)]), ((960, 320), [(768, 512)])]
WIDE = [((0, 640), [(0, 512)]), ((640, 640), [(512, 512), (1024, 256)])]
LAST = [((0, 480), [(0, 256)]), ((480, 480), [(256, 512)]), ((960, 192), [(768, 256), (1024, 128)]), ((1152, 128), [(1152, 128)])]
PIECES = [NARROW, WIDE, WIDE, LAST]


def tile_moe_shr_lin_gelu_kernel(tc, xT, w_words, w_scales, b, gate, offs, pos1, pos2, out):
    nc = tc.nc
    with ExitStack() as ctx:
        keep = ctx.enter_context(tc.tile_pool(name="keep", bufs=1))
        ring = ctx.enter_context(tc.tile_pool(name="ring", bufs=2))
        psum = ctx.enter_context(tc.psum_pool(name="psum", bufs=1))

        offs_t = keep.tile([P, S // 16], U16, name="offs_t")
        pos1_t = keep.tile([P, T // 16], U16, name="pos1_t")
        pos2_t = keep.tile([P, T // 16], U16, name="pos2_t")
        bias = keep.tile([P, E + 1], F32, name="bias")
        gates = keep.tile([P, 2 * T], F32, name="gates")
        wsc = keep.tile([P, (E + 1) * PASSES * N], U8, name="wsc", align_bytes=64)
        warm = keep.tile([P, 8], F32, name="warm")
        y = keep.tile([P, S], F32, name="y")
        ys = keep.tile([P, T], F32, name="ys")
        words, gath, slots, shq, cs, ss, csh, ssh = [], [], [], [], [], [], [], []
        for a in range(PASSES):
            words.append(keep.tile([P, (E + 1) * 2 * N], U8, name=f"words{a}", align_bytes=64))
            gath.append(keep.tile([P, 4 * S], BF16, name=f"gath{a}", align_bytes=64))
            slots.append(keep.tile([P, 4 * S], BF16, name=f"slots{a}", align_bytes=64))
            shq.append(keep.tile([P, 4 * 512], BF16, name=f"shq{a}", align_bytes=64))
            cs.append(keep.tile([P, S], U32, name=f"cs{a}", align_bytes=64))
            ss.append(keep.tile([P, S], U8, name=f"ss{a}", align_bytes=64))
            csh.append(keep.tile([P, 512], U32, name=f"csh{a}", align_bytes=64))
            ssh.append(keep.tile([P, 512], U8, name=f"ssh{a}", align_bytes=64))
        rest = keep.tile([P, PASSES * 4 * C], BF16, name="rest", align_bytes=64)
        crest = keep.tile([P, PASSES * C], U32, name="crest", align_bytes=64)
        srest = keep.tile([P, PASSES * C], U8, name="srest", align_bytes=64)

        pairs_all = keep.tile([P, PASSES * 4 * T], BF16, name="pairs_all", align_bytes=64)
        pairs = [pairs_all[:, 4 * T * (PASSES - 1 - a) : 4 * T * (PASSES - a)] for a in range(PASSES)]

        xv = xT.rearrange("(a p j) t -> a p j t", p=P, j=4)
        wv = w_words.bitcast(I32)
        sv = w_scales.bitcast(I32)

        nc.vector.memset(warm[:], 0.0)
        nc.scalar.activation(out=warm[:], in_=warm[:], func=GELU)
        nc.vector.memset(wsc[:].bitcast(I32), 0)

        raw = {}

        def load_x(a, h):
            raw[a, h] = ring.tile([P, 2, T], F32, name=f"raw{h}")
            nc.sync.dma_start(raw[a, h][:], xv[a][:, 2 * h : 2 * h + 2, :])

        def load_w(a):
            nc.sync.dma_start(
                words[a][:].bitcast(I32).rearrange("p (e n) -> p e n", e=E + 1),
                wv[:, a, :, :].rearrange("e p n -> p e n"),
            )

        load_x(0, 0)
        nc.sync.dma_start(offs_t[:], offs)
        load_x(0, 1)
        load_x(1, 0)
        load_x(1, 1)

        def load_rest():
            load_x(2, 0)
            load_x(2, 1)
            for q in range(4):
                nc.sync.dma_start(
                    wsc[32 * q : 32 * q + 4, :].bitcast(I32).rearrange("q (i n) -> q i n", n=N // 4),
                    sv[:, :, 4 * q : 4 * q + 4, :].rearrange("e a q n -> q (e a) n"),
                )
            load_w(0)
            load_x(3, 0)
            load_x(3, 1)
            load_w(1)
            load_w(2)
            load_w(3)
            nc.sync.dma_start(bias[:], b)
            nc.sync.dma_start(pos1_t[:], pos1)
            nc.sync.dma_start(pos2_t[:], pos2)
            nc.sync.dma_start(gates[:].rearrange("p (g t) -> p g t", g=2), gate.rearrange("g p t -> p g t"))

        def cast(a, h, c0=0, c1=T, copy=nc.scalar.copy):
            copy(
                out=pairs[a][:, 2 * T * h : 2 * T * (h + 1)].rearrange("p (t e) -> p t e", e=2)[:, c0:c1, :],
                in_=raw[a, h][:, :, c0:c1].rearrange("p e t -> p t e"),
            )

        def gather(a, h, start, size):
            window = 2 * T * (PASSES - 1 - a) + T * h
            nc.vector.tensor_copy(
                gath[a][:].bitcast(U32)[:, S * h + start : S * h + start + size],
                pairs_all[:].bitcast(U32)[:, window : window + (T if size < T else 2 * T)].indirect(offs_t[:, start // 16 : (start + size) // 16]),
            )

        def weave(a, start, size):
            nc.scalar.copy(
                out=slots[a][:].bitcast(U32).rearrange("p (n u) -> p n u", u=2)[:, start : start + size, :],
                in_=gath[a][:].bitcast(U32).rearrange("p (u n) -> p n u", u=2)[:, start : start + size, :],
            )

        def weave_shared(a):
            src = pairs[a].bitcast(U32).rearrange("p (u n) -> p n u", u=2)
            nc.scalar.copy(out=shq[a][:].bitcast(U32).rearrange("p (n u) -> p n u", u=2), in_=src[:, :512, :])
            nc.scalar.copy(
                out=rest[:].bitcast(U32)[:, 2 * C * a : 2 * C * (a + 1)].rearrange("p (n u) -> p n u", u=2), in_=src[:, 512:, :]
            )

        def quant(a, cuts):
            for s0, w in cuts:
                nc.vector.quantize_mx(
                    out=cs[a][:, s0 : s0 + w].bitcast(FP8X4),
                    scales=ss[a][:, s0 : s0 + w],
                    in_=slots[a][:, 4 * s0 : 4 * (s0 + w)],
                )

        def quant_shared(a):
            nc.vector.quantize_mx(out=csh[a][:].bitcast(FP8X4), scales=ssh[a][:], in_=shq[a][:])

        def quant_rest():
            nc.vector.quantize_mx(out=crest[:].bitcast(FP8X4), scales=srest[:], in_=rest[:])

        def multiply(bank, e, codes, scales, s0, w):
            for a in range(PASSES):
                i = e * PASSES + a
                nc.tensor.matmul_mx(
                    out=bank,
                    lhsT=words[a][:, e * 2 * N : (e + 1) * 2 * N].bitcast(FP4X4),
                    lhsT_scale=wsc[:, i * N : (i + 1) * N],
                    rhs=codes(a)[:, s0(a) : s0(a) + w].bitcast(FP8X4),
                    rhs_scale=scales(a)[:, s0(a) : s0(a) + w],
                    start=(a == 0),
                    stop=(a == PASSES - 1),
                )

        banks = {}

        def bank_of(e):
            key = e if e > 5 else e // 2
            if key not in banks:
                banks[key] = psum.tile([P, 3 * C if key == 0 else 2 * C if key < 3 else C], F32, name=f"bank{key}")
            at = e % 2 * C if key < 3 else 0
            return banks[key][:, at : at + C]

        def experts(group):
            for e in group:
                multiply(bank_of(e), e, lambda a: cs[a], lambda a: ss[a], lambda a: e * C, C)
            for e in group:
                nc.scalar.activation(out=y[:, e * C : (e + 1) * C], in_=bank_of(e), func=GELU, bias=bias[:, e : e + 1])

        def shared():
            bank = psum.tile([P, 512], F32, name="bank_shared")
            multiply(bank[:], E, lambda a: csh[a], lambda a: ssh[a], lambda a: 0, 512)
            nc.scalar.activation(out=ys[:, :512], in_=bank[:], func=GELU, bias=bias[:, E : E + 1])
            bank_rest = banks[0][:, 2 * C :]
            multiply(bank_rest, E, lambda a: crest, lambda a: srest, lambda a: a * C, C)
            nc.scalar.activation(out=ys[:, 512:], in_=bank_rest, func=GELU, bias=bias[:, E : E + 1])

        cast(0, 0, 0, 384, nc.vector.tensor_copy)
        cast(0, 0, 384, T)
        cast(0, 1)
        cast(1, 0)
        cast(1, 1)
        load_rest()
        pending = []

        def finish(a, cuts):
            quant(a, cuts)
            if a == PASSES - 1:
                for s0, w in cuts:
                    experts(range(s0 // C, (s0 + w) // C))

        for a in range(PASSES):
            if 0 < a < PASSES - 1:
                cast(a + 1, 0)
                cast(a + 1, 1)
            for i, ((start, size), cuts) in enumerate(PIECES[a]):
                gather(a, 0, start, size)
                gather(a, 1, start, size)
                weave(a, start, size)
                if pending:
                    finish(*pending.pop())
                pending.append((a, cuts))
                if i == min(len(PIECES[a]) - 1, 2):
                    weave_shared(a)
        finish(*pending.pop())
        for a in range(PASSES):
            quant_shared(a)
        quant_rest()
        shared()

        s1 = keep.tile([P, T], F32, name="s1")
        s2 = keep.tile([P, T], F32, name="s2")
        t1 = keep.tile([P, T], F32, name="t1")
        res = keep.tile([P, T], F32, name="res")
        nc.vector.tensor_tensor(s1[:], y[:].indirect(pos1_t[:]), gates[:, :T], MULT)
        nc.vector.tensor_tensor(s2[:], y[:].indirect(pos2_t[:]), gates[:, T:], MULT)
        parts = (slice(0, 384), slice(384, T))
        for cols in parts:
            nc.vector.tensor_add(t1[:, cols], s1[:, cols], ys[:, cols])
        for cols in parts:
            nc.vector.tensor_add(res[:, cols], t1[:, cols], s2[:, cols])
            nc.sync.dma_start(out[:, cols], res[:, cols])
